import numpy as np
import ml_dtypes


def mxq(x, axis, fmt="e4m3"):
    dtype, down = {"e4m3": (ml_dtypes.float8_e4m3fn, 7), "e5m2": (ml_dtypes.float8_e5m2, 14)}[fmt]
    v = np.moveaxis(np.asarray(x, np.float32).astype(ml_dtypes.bfloat16).astype(np.float64), axis, -1)
    blocks = v.reshape(v.shape[:-1] + (-1, 32))
    amax = np.abs(blocks).max(-1, keepdims=True)
    byte = np.maximum(np.where(amax > 0, np.frexp(amax)[1] - 1 + 127, 0) - down, 1)
    scale = np.exp2(byte - 127.0)
    codes = (blocks / scale).astype(np.float32).astype(dtype).astype(np.float64)
    return np.moveaxis((codes * scale).reshape(v.shape), -1, axis)


WIDE = False


def mx_kscale(k):
    if not WIDE:
        return np.ones(k)
    levels = np.array([10, -10, 5, -5, 0])
    if k % 512:
        return np.exp2(np.random.permutation(np.resize(levels, k // 32))).repeat(32)
    a = np.empty((k // 512, 16))
    for p in range(k // 512):
        a[p, :8] = np.random.permutation(np.resize(levels, 8))
        for g in range(8):
            far = levels[np.abs(levels - a[p, g]) >= 10]
            a[p, g + 8] = far[np.random.randint(len(far))]
    return np.exp2(a.ravel()).repeat(32)


def f64(x):
    return np.asarray(x).astype(np.float64)


def striped(idx):
    return np.tile(idx.reshape(-1, 16).T, (8, 1)).astype(np.uint16)


def unstriped(offs):
    return offs[:16].T.reshape(-1).astype(np.int64)


def gelu(v):
    return 0.5 * v * (1.0 + np.tanh(np.sqrt(2.0 / np.pi) * (v + 0.044715 * v**3)))


K, T, E, C, N = 1024, 640, 20, 128, 256
TOP = 4


def by_expert(wq, xq):
    return np.concatenate([wq[e].T @ xq[:, e * C:(e + 1) * C] for e in range(E)], axis=1)


def setup_inputs():
    n = np.random.standard_normal
    s = mx_kscale(K)[:, None]
    deal = np.repeat(np.arange(E), C).reshape(TOP, T)[:, np.random.permutation(T)]
    deal = np.take_along_axis(deal, np.argsort(np.random.rand(TOP, T), axis=0), axis=0)
    for _ in range(8):
        s_, t_ = np.random.permutation(T).reshape(2, -1); r = np.random.randint(TOP, size=T // 2); x, y = deal[r, s_].copy(), deal[r, t_].copy()
        ok = ~((deal[:, s_] == y).any(0) | (deal[:, t_] == x).any(0)); deal[r[ok], s_[ok]] = y[ok]; deal[r[ok], t_[ok]] = x[ok]
    order = np.lexsort((np.random.rand(TOP * T), deal.reshape(-1)))
    slot_token = order % T; pos = np.empty(TOP * T, np.int64); pos[order] = np.arange(TOP * T); pos = pos.reshape(TOP, T)
    g = np.random.uniform(0.5, 1.5, (TOP, T)); g = g / g.sum(0)
    return {
        "xT": (n((K, T)) * s).astype(np.float32),
        "w": (n((E + 1, K, N)) / np.sqrt(K) / s[None]).astype(np.float32),
        "b": (0.3 * n((N, E + 1))).astype(np.float32),
        "gate": np.stack([np.tile(r, (N, 1)) for r in g]).astype(np.float32),
        "offs": striped(slot_token),
        "pos1": striped(pos[0]),
        "pos2": striped(pos[1]),
        "pos3": striped(pos[2]),
        "pos4": striped(pos[3]),
    }


def reference(xT, w, b, gate, offs, pos1, pos2, pos3, pos4):
    idx = unstriped(offs)
    wq = mxq(f64(w), 1, "e4m3")
    xs = mxq(f64(xT), 0, "e4m3")
    ys = gelu((wq[E].T @ xs) + f64(b)[:, E:])
    xq = mxq(f64(xT)[:, idx], 0, "e4m3")
    y = by_expert(wq, xq)
    y = gelu(y + np.repeat(f64(b)[:, :E], C, axis=1))
    return ys + sum(f64(gate[r]) * y[:, unstriped(p)] for r, p in enumerate((pos1, pos2, pos3, pos4)))

@@ -1,0 +1,263 @@
+from contextlib import ExitStack
+
+import concourse.mybir as mybir
+
+K, T, E, C, N = 1024, 640, 20, 128, 256
+TOP = 4
+SLOTS = E * C
+FLOPS = 2 * K * N * (SLOTS + T)
+
+F32 = mybir.dt.float32
+BF16 = mybir.dt.bfloat16
+U32 = mybir.dt.uint32
+U16 = mybir.dt.uint16
+U8 = mybir.dt.uint8
+FP8X4 = mybir.dt.float8_e4m3fn_x4
+GELU = mybir.ActivationFunctionType.Gelu_apprx_tanh
+MULT = mybir.AluOpType.mult
+ADD = mybir.AluOpType.add
+
+P = 128
+PASSES = 2
+HALVES = 2
+CHUNK = 512
+CHUNKS = SLOTS // CHUNK
+EXPERTS_PER_CHUNK = CHUNK // C
+WINDOW = 1024
+VECTOR_CASTS = ((8, 1), (11, 1), (14, 1), (16, 1), (18, 1), (19, 1))
+
+
+def tile_moe_shr_lin_gelu_kernel(tc, xT, w, b, gate, offs, pos1, pos2, pos3, pos4, out):
+    nc = tc.nc
+    with ExitStack() as ctx:
+        lists = ctx.enter_context(tc.tile_pool(name="lists", bufs=1))
+        keep = ctx.enter_context(tc.tile_pool(name="keep", bufs=1))
+        wraw_pool = ctx.enter_context(tc.tile_pool(name="wraw", bufs=10))
+        wbf_pool = ctx.enter_context(tc.tile_pool(name="wbf", bufs=4))
+        wq_pool = ctx.enter_context(tc.tile_pool(name="wq", bufs=8))
+        gat_pool = ctx.enter_context(tc.tile_pool(name="gat", bufs=3))
+        psum = ctx.enter_context(tc.psum_pool(name="psum", bufs=4))
+        psum_s = ctx.enter_context(tc.psum_pool(name="psum_s", bufs=1))
+
+        offs_sb = lists.tile([P, SLOTS // 16], U16, name="offs_sb")
+        pos_sb = [lists.tile([P, T // 16], U16, name="pos_sb%d" % r) for r in range(TOP)]
+
+        warm = keep.tile([P, 8], F32, name="warm")
+        warm_out = keep.tile([P, 8], F32, name="warm_out")
+        nc.vector.memset(warm[:], 0.0)
+        nc.scalar.activation(warm_out[:], warm[:], GELU)
+
+        x_raw = [[keep.tile([P, 2, T], F32, name="x_raw%d%d" % (g, u)) for u in range(2)] for g in range(PASSES)]
+        x_bf = [keep.tile([P, 8 * T], BF16, name="x_bf%d" % g, align_bytes=64) for g in range(PASSES)]
+        xs_codes = [keep.tile([P, T], U32, name="xs_codes%d" % g, align_bytes=64) for g in range(PASSES)]
+        xs_scales = [keep.tile([P, T], U8, name="xs_scales%d" % g, align_bytes=64) for g in range(PASSES)]
+        x_codes = [[keep.tile([P, CHUNK], U32, name="x_codes%d%d" % (g, c), align_bytes=64) for c in range(CHUNKS)] for g in range(PASSES)]
+        x_scales = [[keep.tile([P, CHUNK], U8, name="x_scales%d%d" % (g, c), align_bytes=64) for c in range(CHUNKS)] for g in range(PASSES)]
+        bias = keep.tile([P, HALVES, E + 1], F32, name="bias")
+        y = [keep.tile([P, SLOTS], F32, name="y%d" % h) for h in range(HALVES)]
+        ys = [keep.tile([P, T], F32, name="ys%d" % h) for h in range(HALVES)]
+        gate_sb = [[keep.tile([P, T], F32, name="gate%d%d" % (h, r)) for r in range(TOP)] for h in range(HALVES)]
+
+        x_rows = xT.rearrange("(g p u e) t -> g u p e t", g=PASSES, p=P, u=2, e=2)
+        w_rows = w.rearrange("x (g p j) n -> x g p j n", g=PASSES, p=P, j=4)
+        w_raw = {}
+        w_bf = {}
+        w_codes = {}
+        w_scales = {}
+        gathered = {}
+        grouped = {}
+
+        def load_x(g, u):
+            nc.sync.dma_start(x_raw[g][u][:], x_rows[g, u])
+
+        def load_w(e):
+            for g in range(PASSES):
+                w_raw[e, g] = wraw_pool.tile([P, 4, N], F32, name="w_raw")
+                nc.sync.dma_start(w_raw[e, g][:], w_rows[e, g])
+
+        def cast_x(g, u, on_vector):
+            dst = x_bf[g][:, 2 * T * u : 2 * T * (u + 1)].rearrange("p (c i e) -> p c e i", i=4, e=2)
+            src = x_raw[g][u][:].rearrange("p e (c i) -> p c e i", i=4)
+            if on_vector:
+                nc.vector.tensor_copy(dst, src)
+            else:
+                nc.scalar.copy(dst, src)
+
+        def group_shared_x(g):
+            dst = x_bf[g][:, 4 * T : 8 * T].rearrange("p (t u e) -> p t u e", u=2, e=2)
+            src = x_bf[g][:, 0 : 4 * T].rearrange("p (u t e) -> p t u e", u=2, e=2)
+            nc.vector.tensor_copy(dst, src)
+
+        def quantize_shared_x(g):
+            for t0, t1 in ((0, 512), (512, T)):
+                nc.vector.quantize_mx(
+                    out=xs_codes[g][:, t0:t1].bitcast(FP8X4),
+                    scales=xs_scales[g][:, t0:t1],
+                    in_=x_bf[g][:, 4 * T + 4 * t0 : 4 * T + 4 * t1],
+                )
+
+        def gather_x(g, c, u):
+            if u == 0:
+                gathered[g, c] = gat_pool.tile([P, 2, 2 * CHUNK], BF16, name="gathered")
+            window = x_bf[g][:].bitcast(U32)[:, T * u : T * u + WINDOW]
+            columns = offs_sb[:, c * CHUNK // 16 : (c + 1) * CHUNK // 16]
+            nc.vector.tensor_copy(gathered[g, c][:, u, :].bitcast(U32), window.indirect(columns))
+
+        def group_x(g, c):
+            grouped[g, c] = gat_pool.tile([P, 4 * CHUNK], BF16, name="grouped", align_bytes=64)
+            nc.vector.tensor_copy(
+                grouped[g, c][:].rearrange("p (s u e) -> p s u e", u=2, e=2),
+                gathered[g, c][:].rearrange("p u (s e) -> p s u e", e=2),
+            )
+
+        def quantize_x(g, c):
+            nc.vector.quantize_mx(out=x_codes[g][c][:].bitcast(FP8X4), scales=x_scales[g][c][:], in_=grouped[g, c][:])
+
+        def cast_w(e):
+            w_bf[e] = wbf_pool.tile([P, PASSES, 4 * N], BF16, name="w_bf", align_bytes=64)
+            for g in range(PASSES):
+                dst = w_bf[e][:, g, :].rearrange("p (c i j) -> p c j i", i=2, j=4)
+                src = w_raw[e, g][:].rearrange("p j (c i) -> p c j i", i=2)
+                if (e, g) in VECTOR_CASTS:
+                    nc.vector.tensor_copy(dst, src)
+                else:
+                    nc.scalar.copy(dst, src)
+
+        def quantize_w(e):
+            w_codes[e] = wq_pool.tile([P, PASSES * N], U32, name="w_codes", align_bytes=64)
+            w_scales[e] = wq_pool.tile([P, PASSES * N], U8, name="w_scales", align_bytes=64)
+            nc.vector.quantize_mx(
+                out=w_codes[e][:].bitcast(FP8X4),
+                scales=w_scales[e][:],
+                in_=w_bf[e][:].rearrange("p g m -> p (g m)"),
+            )
+
+        def product(acc, e, h, codes, scales, cols):
+            for g in range(PASSES):
+                m = slice(g * N + h * P, g * N + (h + 1) * P)
+                nc.tensor.matmul_mx(
+                    out=acc,
+                    lhsT=w_codes[e][:, m].bitcast(FP8X4),
+                    lhsT_scale=w_scales[e][:, m],
+                    rhs=codes[g][:, cols].bitcast(FP8X4),
+                    rhs_scale=scales[g][:, cols],
+                    start=(g == 0),
+                    stop=(g == PASSES - 1),
+                )
+
+        def expert(e):
+            c, place = divmod(e, EXPERTS_PER_CHUNK)
+            acc = psum.tile([P, HALVES, C], F32, name="acc")
+            codes = [x_codes[g][c] for g in range(PASSES)]
+            scales = [x_scales[g][c] for g in range(PASSES)]
+            for h in range(HALVES):
+                product(acc[:, h, :], e, h, codes, scales, slice(place * C, (place + 1) * C))
+            for h in range(HALVES):
+                nc.scalar.activation(y[h][:, e * C : (e + 1) * C], acc[:, h, :], GELU, bias=bias[:, h, e : e + 1])
+
+        def shared_expert():
+            for h in range(HALVES):
+                for t0, t1 in ((0, 512), (512, T)):
+                    acc_s = psum_s.tile([P, t1 - t0], F32, name="acc_s%d%d" % (h, t0))
+                    product(acc_s[:], E, h, xs_codes, xs_scales, slice(t0, t1))
+                    nc.scalar.activation(ys[h][:, t0:t1], acc_s[:], GELU, bias=bias[:, h, E : E + 1])
+
+        load_x(0, 0)
+        load_x(0, 1)
+        nc.sync.dma_start(offs_sb[:], offs)
+        load_w(0)
+        load_w(1)
+        load_x(1, 0)
+        load_x(1, 1)
+        nc.sync.dma_start(bias[:], b.rearrange("(h p) e -> p h e", p=P))
+
+        cast_x(0, 0, False)
+        cast_x(0, 1, True)
+        group_shared_x(0)
+        cast_w(0)
+        cast_w(1)
+        cast_x(1, 0, False)
+        cast_x(1, 1, False)
+
+        units = [(0, 0), (0, 1), (0, 2), (1, 0), (1, 1), (0, 3), (1, 2), (0, 4), (1, 3), (1, 4)]
+        token_steps = []
+        for i in range(len(units) + 1):
+            step = []
+            if i < len(units):
+                if units[i] == (1, 0):
+                    step.append((group_shared_x, (1,)))
+                step.append((gather_x, units[i] + (0,)))
+            if i >= 1:
+                step.append((group_x, units[i - 1]))
+            if i < len(units):
+                step.append((gather_x, units[i] + (1,)))
+            if i >= 1:
+                step.append((quantize_x, units[i - 1]))
+            token_steps.append(step)
+
+        def run_token_step(i):
+            for fn, args in token_steps[i]:
+                fn(*args)
+
+        for i in range(5):
+            run_token_step(i)
+        next_step = 5
+        quantize_w(0)
+        for e in range(E):
+            if e + 2 < E:
+                load_w(e + 2)
+            if e == 4:
+                for r, p_list in enumerate((pos1, pos2, pos3, pos4)):
+                    nc.sync.dma_start(pos_sb[r][:], p_list)
+            if e + 2 < E:
+                cast_w(e + 2)
+            if e + 1 < E:
+                quantize_w(e + 1)
+            expert(e)
+            if e % 2 == 1 and next_step < len(token_steps):
+                run_token_step(next_step)
+                next_step += 1
+            if e == 14:
+                quantize_shared_x(0)
+            if e == 16:
+                quantize_shared_x(1)
+
+        for r in range(TOP):
+            nc.sync.dma_start(gate_sb[0][r][:], gate[r, 0:P, :])
+        load_w(E)
+        for r in range(TOP):
+            nc.sync.dma_start(gate_sb[1][r][:], gate[r, P : 2 * P, :])
+        cast_w(E)
+
+        prod = [[keep.tile([P, T], F32, name="prod%d%d" % (h, r)) for r in range(TOP)] for h in range(HALVES)]
+
+        def fetch(h, r, t0=0, t1=T):
+            nc.vector.tensor_tensor(
+                prod[h][r][:, t0:t1], y[h][:].indirect(pos_sb[r][:, t0 // 16 : t1 // 16]), gate_sb[h][r][:, t0:t1], MULT
+            )
+
+        def add(dst, a, c, t0=0, t1=T):
+            nc.vector.tensor_tensor(dst[:, t0:t1], a[:, t0:t1], c[:, t0:t1], ADD)
+
+        fetch(0, 0)
+        fetch(0, 1)
+        fetch(0, 2)
+        add(prod[0][0], prod[0][0], prod[0][1])
+        fetch(0, 3)
+        quantize_w(E)
+        shared_expert()
+        add(prod[0][0], prod[0][0], prod[0][2])
+        fetch(1, 0)
+        add(prod[0][0], prod[0][0], prod[0][3])
+        fetch(1, 1)
+        add(prod[0][0], prod[0][0], ys[0])
+        nc.sync.dma_start(out[0:P, :], prod[0][0][:])
+        fetch(1, 2)
+        add(prod[1][0], prod[1][0], prod[1][1])
+        add(prod[1][2], prod[1][2], ys[1])
+        fetch(1, 3, 0, T // 2)
+        add(prod[1][0], prod[1][0], prod[1][2])
+        fetch(1, 3, T // 2, T)
+        for t0 in (0, T // 2):
+            add(prod[1][0], prod[1][0], prod[1][3], t0, t0 + T // 2)
+            nc.sync.dma_start(out[P : 2 * P, t0 : t0 + T // 2], prod[1][0][:, t0 : t0 + T // 2])

@@ -1,6 +1,7 @@
 from contextlib import ExitStack
 
 import concourse.mybir as mybir
+from concourse.masks import make_identity
 
 K, T, E, C, N = 1024, 640, 20, 128, 256
 TOP = 4
@@ -24,7 +25,13 @@ CHUNK = 512
 CHUNKS = SLOTS // CHUNK
 EXPERTS_PER_CHUNK = CHUNK // C
 WINDOW = 1024
-VECTOR_CASTS = ((8, 1), (11, 1), (14, 1), (16, 1), (18, 1), (19, 1))
+RING = 8
+FETCH_ORDER = ((1, 0), (1, 1), (1, 2), (0, 0), (0, 1), (0, 2), (1, 3), (0, 3))
+PLANE_TILES = 3
+VECTOR_CASTS = ((18, 0), (18, 1), (19, 0), (19, 1))
+UNITS = ((0, 0), (0, 1), (1, 0), (1, 1), (0, 2), (1, 2), (0, 3), (1, 3), (0, 4), (1, 4))
+PACE = (2, 3, 6, 8, 9, 10, 12, 14, 15)
+PRODUCT_AFTER = (7, 8, 8, 8, 9, 9, 11, 11, 13, 13, 14, 15, 17, 17, 17, 17, 18, 18, 18, 19)
 
 
 def tile_moe_shr_lin_gelu_kernel(tc, xT, w, b, gate, offs, pos1, pos2, pos3, pos4, out):
@@ -32,12 +39,9 @@ def tile_moe_shr_lin_gelu_kernel(tc, xT, w, b, gate, offs, pos1, pos2, pos3, pos
     with ExitStack() as ctx:
         lists = ctx.enter_context(tc.tile_pool(name="lists", bufs=1))
         keep = ctx.enter_context(tc.tile_pool(name="keep", bufs=1))
-        wraw_pool = ctx.enter_context(tc.tile_pool(name="wraw", bufs=10))
-        wbf_pool = ctx.enter_context(tc.tile_pool(name="wbf", bufs=4))
-        wq_pool = ctx.enter_context(tc.tile_pool(name="wq", bufs=8))
-        gat_pool = ctx.enter_context(tc.tile_pool(name="gat", bufs=3))
-        psum = ctx.enter_context(tc.psum_pool(name="psum", bufs=4))
-        psum_s = ctx.enter_context(tc.psum_pool(name="psum_s", bufs=1))
+        wbf_pool = ctx.enter_context(tc.tile_pool(name="wbf", bufs=6))
+        wq_pool = ctx.enter_context(tc.tile_pool(name="wq", bufs=4 * PLANE_TILES))
+        psum = ctx.enter_context(tc.psum_pool(name="psum", bufs=8))
 
         offs_sb = lists.tile([P, SLOTS // 16], U16, name="offs_sb")
         pos_sb = [lists.tile([P, T // 16], U16, name="pos_sb%d" % r) for r in range(TOP)]
@@ -46,34 +50,43 @@ def tile_moe_shr_lin_gelu_kernel(tc, xT, w, b, gate, offs, pos1, pos2, pos3, pos
         warm_out = keep.tile([P, 8], F32, name="warm_out")
         nc.vector.memset(warm[:], 0.0)
         nc.scalar.activation(warm_out[:], warm[:], GELU)
+        ident = keep.tile([P, P], F32, name="ident")
+        make_identity(nc, ident[:])
 
         x_raw = [[keep.tile([P, 2, T], F32, name="x_raw%d%d" % (g, u)) for u in range(2)] for g in range(PASSES)]
         x_bf = [keep.tile([P, 8 * T], BF16, name="x_bf%d" % g, align_bytes=64) for g in range(PASSES)]
-        xs_codes = [keep.tile([P, T], U32, name="xs_codes%d" % g, align_bytes=64) for g in range(PASSES)]
-        xs_scales = [keep.tile([P, T], U8, name="xs_scales%d" % g, align_bytes=64) for g in range(PASSES)]
         x_codes = [[keep.tile([P, CHUNK], U32, name="x_codes%d%d" % (g, c), align_bytes=64) for c in range(CHUNKS)] for g in range(PASSES)]
         x_scales = [[keep.tile([P, CHUNK], U8, name="x_scales%d%d" % (g, c), align_bytes=64) for c in range(CHUNKS)] for g in range(PASSES)]
         bias = keep.tile([P, HALVES, E + 1], F32, name="bias")
         y = [keep.tile([P, SLOTS], F32, name="y%d" % h) for h in range(HALVES)]
         ys = [keep.tile([P, T], F32, name="ys%d" % h) for h in range(HALVES)]
-        gate_sb = [[keep.tile([P, T], F32, name="gate%d%d" % (h, r)) for r in range(TOP)] for h in range(HALVES)]
+        ring = [keep.tile([P, PASSES * 4 * N], F32, name="ring%d" % i, align_bytes=64) for i in range(RING)]
+        first = [keep.tile([P, PASSES * 4 * N], F32, name="first%d" % i, align_bytes=64) for i in range(2)]
+        prod = [[x_raw[h][r // 2][:, r % 2, :] for r in range(TOP)] for h in range(HALVES)]
 
+        xs_codes = [keep.tile([P, T], U32, name="xs_codes%d" % g, align_bytes=64) for g in range(PASSES)]
+        spare = [first[1], ring[(E - 8) % RING], ring[(E - 7) % RING]]
+        gate_sb = {}
+        for i, (h, r) in enumerate(FETCH_ORDER):
+            gate_sb[h, r] = spare[i // 3][:, i % 3 * T : (i % 3 + 1) * T]
         x_rows = xT.rearrange("(g p u e) t -> g u p e t", g=PASSES, p=P, u=2, e=2)
-        w_rows = w.rearrange("x (g p j) n -> x g p j n", g=PASSES, p=P, j=4)
-        w_raw = {}
+        w_rows = w.rearrange("x (g p j) n -> x g p (j n)", g=PASSES, p=P, j=4)
+        planes = [keep.tile([P, T], U8, name="planes%d" % i, align_bytes=64) for i in range(PLANE_TILES)]
+        xs_scales = [planes[E % PLANE_TILES][4 * g :, :] for g in range(PASSES)]
         w_bf = {}
         w_codes = {}
         w_scales = {}
-        gathered = {}
-        grouped = {}
 
         def load_x(g, u):
             nc.sync.dma_start(x_raw[g][u][:], x_rows[g, u])
 
+        def w_raw(e, g):
+            home = ring[e % RING] if e < E else first[0]
+            return home[:, g * 4 * N : (g + 1) * 4 * N]
+
         def load_w(e):
             for g in range(PASSES):
-                w_raw[e, g] = wraw_pool.tile([P, 4, N], F32, name="w_raw")
-                nc.sync.dma_start(w_raw[e, g][:], w_rows[e, g])
+                nc.sync.dma_start(w_raw(e, g), w_rows[e, g])
 
         def cast_x(g, u, on_vector):
             dst = x_bf[g][:, 2 * T * u : 2 * T * (u + 1)].rearrange("p (c i e) -> p c e i", i=4, e=2)
@@ -96,28 +109,37 @@ def tile_moe_shr_lin_gelu_kernel(tc, xT, w, b, gate, offs, pos1, pos2, pos3, pos
                     in_=x_bf[g][:, 4 * T + 4 * t0 : 4 * T + 4 * t1],
                 )
 
-        def gather_x(g, c, u):
-            if u == 0:
-                gathered[g, c] = gat_pool.tile([P, 2, 2 * CHUNK], BF16, name="gathered")
-            window = x_bf[g][:].bitcast(U32)[:, T * u : T * u + WINDOW]
-            columns = offs_sb[:, c * CHUNK // 16 : (c + 1) * CHUNK // 16]
-            nc.vector.tensor_copy(gathered[g, c][:, u, :].bitcast(U32), window.indirect(columns))
+        def gathered(k):
+            home = first[k] if k < 2 else ring[PACE[k - 2] % RING]
+            return home[:].rearrange("p (q m) -> p q m", q=4)[:, 0:4:3, :]
 
-        def group_x(g, c):
-            grouped[g, c] = gat_pool.tile([P, 4 * CHUNK], BF16, name="grouped", align_bytes=64)
+        def grouped(k):
+            home = first[1 - k] if k < 1 else ring[PACE[k - 1] % RING]
+            return home[:, CHUNK : 3 * CHUNK].bitcast(BF16)
+
+        def gather_x(k, u, pieces, width):
+            g, c = UNITS[k]
+            window = x_bf[g][:].bitcast(U32)[:, T * u : T * u + width]
+            size = CHUNK // pieces
+            for s0 in range(0, CHUNK, size):
+                columns = offs_sb[:, (c * CHUNK + s0) // 16 : (c * CHUNK + s0 + size) // 16]
+                nc.vector.tensor_copy(gathered(k)[:, u, s0 : s0 + size].bitcast(U32), window.indirect(columns))
+
+        def group_x(k):
             nc.vector.tensor_copy(
-                grouped[g, c][:].rearrange("p (s u e) -> p s u e", u=2, e=2),
-                gathered[g, c][:].rearrange("p u (s e) -> p s u e", e=2),
+                grouped(k).rearrange("p (s u e) -> p s u e", u=2, e=2),
+                gathered(k).bitcast(BF16).rearrange("p u (s e) -> p s u e", e=2),
             )
 
-        def quantize_x(g, c):
-            nc.vector.quantize_mx(out=x_codes[g][c][:].bitcast(FP8X4), scales=x_scales[g][c][:], in_=grouped[g, c][:])
+        def quantize_x(k):
+            g, c = UNITS[k]
+            nc.vector.quantize_mx(out=x_codes[g][c][:].bitcast(FP8X4), scales=x_scales[g][c][:], in_=grouped(k))
 
         def cast_w(e):
             w_bf[e] = wbf_pool.tile([P, PASSES, 4 * N], BF16, name="w_bf", align_bytes=64)
             for g in range(PASSES):
                 dst = w_bf[e][:, g, :].rearrange("p (c i j) -> p c j i", i=2, j=4)
-                src = w_raw[e, g][:].rearrange("p j (c i) -> p c j i", i=2)
+                src = w_raw(e, g).rearrange("p (j c i) -> p c j i", j=4, i=2)
                 if (e, g) in VECTOR_CASTS:
                     nc.vector.tensor_copy(dst, src)
                 else:
@@ -125,10 +147,10 @@ def tile_moe_shr_lin_gelu_kernel(tc, xT, w, b, gate, offs, pos1, pos2, pos3, pos
 
         def quantize_w(e):
             w_codes[e] = wq_pool.tile([P, PASSES * N], U32, name="w_codes", align_bytes=64)
-            w_scales[e] = wq_pool.tile([P, PASSES * N], U8, name="w_scales", align_bytes=64)
+            w_scales[e] = planes[e % PLANE_TILES][4 * (e // PLANE_TILES % 4) :, 0 : PASSES * N]
             nc.vector.quantize_mx(
                 out=w_codes[e][:].bitcast(FP8X4),
-                scales=w_scales[e][:],
+                scales=w_scales[e],
                 in_=w_bf[e][:].rearrange("p g m -> p (g m)"),
             )
 
@@ -147,7 +169,7 @@ def tile_moe_shr_lin_gelu_kernel(tc, xT, w, b, gate, offs, pos1, pos2, pos3, pos
 
         def expert(e):
             c, place = divmod(e, EXPERTS_PER_CHUNK)
-            acc = psum.tile([P, HALVES, C], F32, name="acc")
+            acc = psum.tile([P, 4, C], F32, name="acc", tag="bank")
             codes = [x_codes[g][c] for g in range(PASSES)]
             scales = [x_scales[g][c] for g in range(PASSES)]
             for h in range(HALVES):
@@ -158,106 +180,111 @@ def tile_moe_shr_lin_gelu_kernel(tc, xT, w, b, gate, offs, pos1, pos2, pos3, pos
         def shared_expert():
             for h in range(HALVES):
                 for t0, t1 in ((0, 512), (512, T)):
-                    acc_s = psum_s.tile([P, t1 - t0], F32, name="acc_s%d%d" % (h, t0))
-                    product(acc_s[:], E, h, xs_codes, xs_scales, slice(t0, t1))
-                    nc.scalar.activation(ys[h][:, t0:t1], acc_s[:], GELU, bias=bias[:, h, E : E + 1])
+                    acc_s = psum.tile([P, 512], F32, name="acc_s", tag="bank")
+                    product(acc_s[:, 0 : t1 - t0], E, h, xs_codes, xs_scales, slice(t0, t1))
+                    nc.scalar.activation(ys[h][:, t0:t1], acc_s[:, 0 : t1 - t0], GELU, bias=bias[:, h, E : E + 1])
 
         load_x(0, 0)
-        load_x(0, 1)
         nc.sync.dma_start(offs_sb[:], offs)
+        load_x(0, 1)
         load_w(0)
         load_w(1)
         load_x(1, 0)
         load_x(1, 1)
         nc.sync.dma_start(bias[:], b.rearrange("(h p) e -> p h e", p=P))
+        for e in range(2, RING):
+            load_w(e)
 
-        cast_x(0, 0, False)
-        cast_x(0, 1, True)
-        group_shared_x(0)
+        cast_x(0, 0, True)
+        cast_x(0, 1, False)
+        gather_x(0, 0, 2, T)
         cast_w(0)
         cast_w(1)
         cast_x(1, 0, False)
         cast_x(1, 1, False)
-
-        units = [(0, 0), (0, 1), (0, 2), (1, 0), (1, 1), (0, 3), (1, 2), (0, 4), (1, 3), (1, 4)]
-        token_steps = []
-        for i in range(len(units) + 1):
-            step = []
-            if i < len(units):
-                if units[i] == (1, 0):
-                    step.append((group_shared_x, (1,)))
-                step.append((gather_x, units[i] + (0,)))
-            if i >= 1:
-                step.append((group_x, units[i - 1]))
-            if i < len(units):
-                step.append((gather_x, units[i] + (1,)))
-            if i >= 1:
-                step.append((quantize_x, units[i - 1]))
-            token_steps.append(step)
-
-        def run_token_step(i):
-            for fn, args in token_steps[i]:
-                fn(*args)
-
-        for i in range(5):
-            run_token_step(i)
-        next_step = 5
+        gather_x(0, 1, 2, T)
+        group_shared_x(0)
+        gather_x(1, 0, 1, WINDOW)
+        group_x(0)
         quantize_w(0)
-        for e in range(E):
-            if e + 2 < E:
-                load_w(e + 2)
+        gather_x(1, 1, 1, WINDOW)
+        quantize_x(0)
+        quantize_w(1)
+        group_shared_x(1)
+
+        loaded = RING
+        for e in range(2, E):
+            cast_w(e)
+            k = PACE.index(e) + 2 if e in PACE else None
+            if k is not None and k < len(UNITS):
+                gather_x(k, 0, 1, WINDOW)
+            quantize_w(e)
+            if k is not None:
+                group_x(k - 1)
+                if k < len(UNITS):
+                    gather_x(k, 1, 1, WINDOW)
+                quantize_x(k - 1)
+            for j in range(E):
+                if PRODUCT_AFTER[j] == e:
+                    assert j <= e < j + 4 * PLANE_TILES and all(PACE[k - 1] <= e for k in range(1, len(UNITS)) if UNITS[k][1] == j // EXPERTS_PER_CHUNK)
+                    expert(j)
+            while loaded < E:
+                old = loaded - RING
+                last_use = PACE[min(PACE.index(old) + 1, len(PACE) - 1)] if old in PACE else old
+                if last_use > e:
+                    break
+                load_w(loaded)
+                loaded += 1
             if e == 4:
                 for r, p_list in enumerate((pos1, pos2, pos3, pos4)):
                     nc.sync.dma_start(pos_sb[r][:], p_list)
-            if e + 2 < E:
-                cast_w(e + 2)
-            if e + 1 < E:
-                quantize_w(e + 1)
-            expert(e)
-            if e % 2 == 1 and next_step < len(token_steps):
-                run_token_step(next_step)
-                next_step += 1
-            if e == 14:
-                quantize_shared_x(0)
-            if e == 16:
-                quantize_shared_x(1)
 
-        for r in range(TOP):
-            nc.sync.dma_start(gate_sb[0][r][:], gate[r, 0:P, :])
-        load_w(E)
-        for r in range(TOP):
-            nc.sync.dma_start(gate_sb[1][r][:], gate[r, P : 2 * P, :])
-        cast_w(E)
+        def load_gate(h, r):
+            nc.sync.dma_start(gate_sb[h, r], gate[r, h * P : (h + 1) * P, :])
 
-        prod = [[keep.tile([P, T], F32, name="prod%d%d" % (h, r)) for r in range(TOP)] for h in range(HALVES)]
-
-        def fetch(h, r, t0=0, t1=T):
+        def fetch(h, r, t0, t1):
             nc.vector.tensor_tensor(
-                prod[h][r][:, t0:t1], y[h][:].indirect(pos_sb[r][:, t0 // 16 : t1 // 16]), gate_sb[h][r][:, t0:t1], MULT
+                prod[h][r][:, t0:t1], y[h][:].indirect(pos_sb[r][:, t0 // 16 : t1 // 16]), gate_sb[h, r][:, t0:t1], MULT
             )
 
-        def add(dst, a, c, t0=0, t1=T):
-            nc.vector.tensor_tensor(dst[:, t0:t1], a[:, t0:t1], c[:, t0:t1], ADD)
+        def add(dst, a, c):
+            nc.vector.tensor_tensor(dst, a, c, ADD)
 
-        fetch(0, 0)
-        fetch(0, 1)
-        fetch(0, 2)
-        add(prod[0][0], prod[0][0], prod[0][1])
-        fetch(0, 3)
+        def turned_sum(terms, turned):
+            banks = []
+            for t0, t1 in ((0, 512), (512, T)):
+                acc_t = psum.tile([P, 512], F32, name="acc_t", tag="bank")
+                for t in range(t0, t1, P):
+                    for i, term in enumerate(terms):
+                        nc.tensor.matmul(
+                            acc_t[:, t - t0 : t - t0 + P], term[:, t : t + P], ident[:],
+                            start=(i == 0), stop=(i == len(terms) - 1), is_transpose=True,
+                        )
+                nc.scalar.copy(turned[:, t0:t1], acc_t[:, 0 : t1 - t0])
+                back = psum.tile([P, 512], F32, name="back", tag="bank")
+                for t in range(t0, t1, P):
+                    nc.tensor.transpose(back[:, t - t0 : t - t0 + P], turned[:, t : t + P], ident[:])
+                banks.append(back)
+            return banks
+
+        for i, (h, r) in enumerate(FETCH_ORDER):
+            if i == 0:
+                load_w(E)
+            load_gate(h, r)
+        quantize_shared_x(0)
+        quantize_shared_x(1)
+        cast_w(E)
         quantize_w(E)
         shared_expert()
-        add(prod[0][0], prod[0][0], prod[0][2])
-        fetch(1, 0)
-        add(prod[0][0], prod[0][0], prod[0][3])
-        fetch(1, 1)
-        add(prod[0][0], prod[0][0], ys[0])
-        nc.sync.dma_start(out[0:P, :], prod[0][0][:])
-        fetch(1, 2)
-        add(prod[1][0], prod[1][0], prod[1][1])
-        add(prod[1][2], prod[1][2], ys[1])
-        fetch(1, 3, 0, T // 2)
-        add(prod[1][0], prod[1][0], prod[1][2])
-        fetch(1, 3, T // 2, T)
-        for t0 in (0, T // 2):
-            add(prod[1][0], prod[1][0], prod[1][3], t0, t0 + T // 2)
-            nc.sync.dma_start(out[P : 2 * P, t0 : t0 + T // 2], prod[1][0][:, t0 : t0 + T // 2])
+        back = {}
+        for h in (1, 0):
+            for r in range(TOP - 1):
+                fetch(h, r, 0, T)
+            back[h] = turned_sum([ys[h], prod[h][2], prod[h][1], prod[h][0]] if h == 1 else [prod[h][2], prod[h][1], prod[h][0], ys[h]], ring[(E - 6 + h) % RING])
+        for h in (1, 0):
+            for t0, t1 in ((0, T),) if h == 1 else ((0, 512), (512, T)):
+                fetch(h, TOP - 1, t0, t1)
+        for h in (1, 0):
+            for (t0, t1), bank in zip(((0, 512), (512, T)), back[h]):
+                add(ys[h][:, t0:t1], bank[:, 0 : t1 - t0], prod[h][3][:, t0:t1])
+                nc.sync.dma_start(out[h * P : (h + 1) * P, t0:t1], ys[h][:, t0:t1])

@@ -26,12 +26,13 @@ CHUNKS = SLOTS // CHUNK
 EXPERTS_PER_CHUNK = CHUNK // C
 WINDOW = 1024
 RING = 8
+TOKEN_RANGES = ((0, 512), (512, T))
 FETCH_ORDER = ((1, 0), (1, 1), (1, 2), (0, 0), (0, 1), (0, 2), (1, 3), (0, 3))
 PLANE_TILES = 3
-VECTOR_CASTS = ((18, 0), (18, 1), (19, 0), (19, 1))
+VECTOR_CASTS = ((13, 0), (18, 0), (18, 1), (19, 0), (19, 1))
 UNITS = ((0, 0), (0, 1), (1, 0), (1, 1), (0, 2), (1, 2), (0, 3), (1, 3), (0, 4), (1, 4))
-PACE = (2, 3, 6, 8, 9, 10, 12, 14, 15)
-PRODUCT_AFTER = (7, 8, 8, 8, 9, 9, 11, 11, 13, 13, 14, 15, 17, 17, 17, 17, 18, 18, 18, 19)
+PACE = (2, 4, 6, 7, 9, 10, 11, 15, 16)
+PRODUCT_AFTER = (7, 7, 9, 9, 9, 9, 9, 10, 14, 17, 17, 17, 17, 17, 17, 17, 18, 18, 19, 19)
 
 
 def tile_moe_shr_lin_gelu_kernel(tc, xT, w, b, gate, offs, pos1, pos2, pos3, pos4, out):
@@ -41,7 +42,8 @@ def tile_moe_shr_lin_gelu_kernel(tc, xT, w, b, gate, offs, pos1, pos2, pos3, pos
         keep = ctx.enter_context(tc.tile_pool(name="keep", bufs=1))
         wbf_pool = ctx.enter_context(tc.tile_pool(name="wbf", bufs=6))
         wq_pool = ctx.enter_context(tc.tile_pool(name="wq", bufs=4 * PLANE_TILES))
-        psum = ctx.enter_context(tc.psum_pool(name="psum", bufs=8))
+        psum = ctx.enter_context(tc.psum_pool(name="psum", bufs=1))
+        bank = [psum.tile([P, 512], F32, name="bank%d" % i) for i in range(8)]
 
         offs_sb = lists.tile([P, SLOTS // 16], U16, name="offs_sb")
         pos_sb = [lists.tile([P, T // 16], U16, name="pos_sb%d" % r) for r in range(TOP)]
@@ -138,8 +140,8 @@ def tile_moe_shr_lin_gelu_kernel(tc, xT, w, b, gate, offs, pos1, pos2, pos3, pos
         def cast_w(e):
             w_bf[e] = wbf_pool.tile([P, PASSES, 4 * N], BF16, name="w_bf", align_bytes=64)
             for g in range(PASSES):
-                dst = w_bf[e][:, g, :].rearrange("p (c i j) -> p c j i", i=2, j=4)
-                src = w_raw(e, g).rearrange("p (j c i) -> p c j i", j=4, i=2)
+                dst = w_bf[e][:, g, :].rearrange("p (c i j) -> p c j i", i=4, j=4)
+                src = w_raw(e, g).rearrange("p (j c i) -> p c j i", j=4, i=4)
                 if (e, g) in VECTOR_CASTS:
                     nc.vector.tensor_copy(dst, src)
                 else:
@@ -169,7 +171,7 @@ def tile_moe_shr_lin_gelu_kernel(tc, xT, w, b, gate, offs, pos1, pos2, pos3, pos
 
         def expert(e):
             c, place = divmod(e, EXPERTS_PER_CHUNK)
-            acc = psum.tile([P, 4, C], F32, name="acc", tag="bank")
+            acc = bank[e % 8][:].rearrange("p (h c) -> p h c", c=C)
             codes = [x_codes[g][c] for g in range(PASSES)]
             scales = [x_scales[g][c] for g in range(PASSES)]
             for h in range(HALVES):
@@ -178,9 +180,9 @@ def tile_moe_shr_lin_gelu_kernel(tc, xT, w, b, gate, offs, pos1, pos2, pos3, pos
                 nc.scalar.activation(y[h][:, e * C : (e + 1) * C], acc[:, h, :], GELU, bias=bias[:, h, e : e + 1])
 
         def shared_expert():
-            for h in range(HALVES):
-                for t0, t1 in ((0, 512), (512, T)):
-                    acc_s = psum.tile([P, 512], F32, name="acc_s", tag="bank")
+            for h in (1, 0):
+                for i, (t0, t1) in enumerate(TOKEN_RANGES):
+                    acc_s = bank[4 + 2 * (1 - h) + i]
                     product(acc_s[:, 0 : t1 - t0], E, h, xs_codes, xs_scales, slice(t0, t1))
                     nc.scalar.activation(ys[h][:, t0:t1], acc_s[:, 0 : t1 - t0], GELU, bias=bias[:, h, E : E + 1])
 
@@ -250,22 +252,19 @@ def tile_moe_shr_lin_gelu_kernel(tc, xT, w, b, gate, offs, pos1, pos2, pos3, pos
         def add(dst, a, c):
             nc.vector.tensor_tensor(dst, a, c, ADD)
 
-        def turned_sum(terms, turned):
-            banks = []
-            for t0, t1 in ((0, 512), (512, T)):
-                acc_t = psum.tile([P, 512], F32, name="acc_t", tag="bank")
+        def add_turned(sums, term, first_term, last_term):
+            for (t0, t1), acc_t in zip(TOKEN_RANGES, sums):
                 for t in range(t0, t1, P):
-                    for i, term in enumerate(terms):
-                        nc.tensor.matmul(
-                            acc_t[:, t - t0 : t - t0 + P], term[:, t : t + P], ident[:],
-                            start=(i == 0), stop=(i == len(terms) - 1), is_transpose=True,
-                        )
+                    nc.tensor.matmul(
+                        acc_t[:, t - t0 : t - t0 + P], term[:, t : t + P], ident[:],
+                        start=first_term and t == t0, stop=last_term and t == t1 - P, is_transpose=True,
+                    )
+
+        def turn_back(sums, turned, back):
+            for (t0, t1), acc_t, total in zip(TOKEN_RANGES, sums, back):
                 nc.scalar.copy(turned[:, t0:t1], acc_t[:, 0 : t1 - t0])
-                back = psum.tile([P, 512], F32, name="back", tag="bank")
                 for t in range(t0, t1, P):
-                    nc.tensor.transpose(back[:, t - t0 : t - t0 + P], turned[:, t : t + P], ident[:])
-                banks.append(back)
-            return banks
+                    nc.tensor.transpose(total[:, t - t0 : t - t0 + P], turned[:, t : t + P], ident[:])
 
         for i, (h, r) in enumerate(FETCH_ORDER):
             if i == 0:
@@ -276,15 +275,19 @@ def tile_moe_shr_lin_gelu_kernel(tc, xT, w, b, gate, offs, pos1, pos2, pos3, pos
         cast_w(E)
         quantize_w(E)
         shared_expert()
-        back = {}
+        back = {1: (bank[4], bank[5]), 0: (bank[6], bank[7])}
         for h in (1, 0):
+            sums = (bank[2 * h], bank[2 * h + 1])
+            terms = [prod[h][0], prod[h][1], prod[h][2], ys[h]] if h == 1 else [prod[h][0], ys[h], prod[h][1], prod[h][2]]
             for r in range(TOP - 1):
                 fetch(h, r, 0, T)
-            back[h] = turned_sum([ys[h], prod[h][2], prod[h][1], prod[h][0]] if h == 1 else [prod[h][2], prod[h][1], prod[h][0], ys[h]], ring[(E - 6 + h) % RING])
+            for i, term in enumerate(terms):
+                add_turned(sums, term, i == 0, i == len(terms) - 1)
+            turn_back(sums, ring[(E - 6 + h) % RING], back[h])
+        fetch(1, TOP - 1, 0, T)
+        for t0, t1 in TOKEN_RANGES:
+            fetch(0, TOP - 1, t0, t1)
         for h in (1, 0):
-            for t0, t1 in ((0, T),) if h == 1 else ((0, 512), (512, T)):
-                fetch(h, TOP - 1, t0, t1)
-        for h in (1, 0):
-            for (t0, t1), bank in zip(((0, 512), (512, T)), back[h]):
-                add(ys[h][:, t0:t1], bank[:, 0 : t1 - t0], prod[h][3][:, t0:t1])
+            for (t0, t1), total in zip(TOKEN_RANGES, back[h]):
+                add(ys[h][:, t0:t1], total[:, 0 : t1 - t0], prod[h][3][:, t0:t1])
                 nc.sync.dma_start(out[h * P : (h + 1) * P, t0:t1], ys[h][:, t0:t1])

@@ -6,6 +6,7 @@ from concourse.masks import make_identity
 K, T, E, C, N = 1024, 640, 20, 128, 256
 TOP = 4
 SLOTS = E * C
+SHARED = E
 FLOPS = 2 * K * N * (SLOTS + T)
 
 F32 = mybir.dt.float32
@@ -19,34 +20,55 @@ MULT = mybir.AluOpType.mult
 ADD = mybir.AluOpType.add
 
 P = 128
-PASSES = 2
-HALVES = 2
+PACK = 4
+PASSES = K // (P * PACK)
+HALVES = N // P
+LIST_COLUMN = 16
+BANKS = 8
+BANK = 512
+TOKEN_RANGES = ((0, BANK), (BANK, T))
+
 CHUNK = 512
-CHUNKS = SLOTS // CHUNK
-EXPERTS_PER_CHUNK = CHUNK // C
-WINDOW = 1024
-RING = 8
-TOKEN_RANGES = ((0, 512), (512, T))
-FETCH_ORDER = ((1, 0), (1, 1), (1, 2), (0, 0), (0, 1), (0, 2), (1, 3), (0, 3))
-PLANE_TILES = 3
-VECTOR_CASTS = ((13, 0), (18, 0), (18, 1), (19, 0), (19, 1))
+CHUNK_EXPERTS = CHUNK // C
+WIDE_WINDOW = 1024
 UNITS = ((0, 0), (0, 1), (1, 0), (1, 1), (0, 2), (1, 2), (0, 3), (1, 3), (0, 4), (1, 4))
-PACE = (2, 4, 6, 7, 9, 10, 11, 15, 16)
-PRODUCT_AFTER = (7, 7, 9, 9, 9, 9, 9, 10, 14, 17, 17, 17, 17, 17, 17, 17, 18, 18, 19, 19)
+EARLY_UNITS = 2
+
+RING = 8
+BF16_BUFFERS = 6
+SCALE_TILES = 3
+PACE = (2, 4, 5, 6, 9, 10, 11, 12, 18)
+VECTOR_ROUNDS = ((2, 0), (9, 1), (11, 1), (12, 1), (18, 0))
+BIAS_AFTER = (10, 11, 16, 19, 19)
+LATE = E - BANKS
+LISTS_AFTER = 4
+FETCH_ORDER = ((1, 0), (1, 1), (1, 2), (0, 0), (0, 1), (0, 2), (1, 3), (0, 3))
+SHARED_BEFORE_GATE = 1
+LATE_BIAS_BEFORE_GATE = 2
 
 
 def tile_moe_shr_lin_gelu_kernel(tc, xT, w, b, gate, offs, pos1, pos2, pos3, pos4, out):
     nc = tc.nc
+
+    chunk_ready = [max(PACE[u - 1] for u in range(1, len(UNITS)) if UNITS[u][1] == c) for c in range(SLOTS // CHUNK)]
+    product_step = []
+    gelu_step = []
+    for j in range(E):
+        bank_free = gelu_step[j - BANKS] + 1 if j >= BANKS else 0
+        product_step.append(max(j, chunk_ready[j // CHUNK_EXPERTS], bank_free))
+        gelu_step.append(max(product_step[j], BIAS_AFTER[j // CHUNK_EXPERTS]))
+    assert max(gelu_step) < E and all(product_step[j] < j + 4 * SCALE_TILES for j in range(E))
+
     with ExitStack() as ctx:
         lists = ctx.enter_context(tc.tile_pool(name="lists", bufs=1))
         keep = ctx.enter_context(tc.tile_pool(name="keep", bufs=1))
-        wbf_pool = ctx.enter_context(tc.tile_pool(name="wbf", bufs=6))
-        wq_pool = ctx.enter_context(tc.tile_pool(name="wq", bufs=4 * PLANE_TILES))
+        wbf_pool = ctx.enter_context(tc.tile_pool(name="wbf", bufs=BF16_BUFFERS))
+        wq_pool = ctx.enter_context(tc.tile_pool(name="wq", bufs=4 * SCALE_TILES))
         psum = ctx.enter_context(tc.psum_pool(name="psum", bufs=1))
-        bank = [psum.tile([P, 512], F32, name="bank%d" % i) for i in range(8)]
+        bank = [psum.tile([P, BANK], F32, name="bank%d" % i) for i in range(BANKS)]
 
-        offs_sb = lists.tile([P, SLOTS // 16], U16, name="offs_sb")
-        pos_sb = [lists.tile([P, T // 16], U16, name="pos_sb%d" % r) for r in range(TOP)]
+        offs_sb = lists.tile([P, SLOTS // LIST_COLUMN], U16, name="offs_sb")
+        pos_sb = [lists.tile([P, T // LIST_COLUMN], U16, name="pos_sb%d" % r) for r in range(TOP)]
 
         warm = keep.tile([P, 8], F32, name="warm")
         warm_out = keep.tile([P, 8], F32, name="warm_out")
@@ -56,104 +78,125 @@ def tile_moe_shr_lin_gelu_kernel(tc, xT, w, b, gate, offs, pos1, pos2, pos3, pos
         make_identity(nc, ident[:])
 
         x_raw = [[keep.tile([P, 2, T], F32, name="x_raw%d%d" % (g, u)) for u in range(2)] for g in range(PASSES)]
-        x_bf = [keep.tile([P, 8 * T], BF16, name="x_bf%d" % g, align_bytes=64) for g in range(PASSES)]
-        x_codes = [[keep.tile([P, CHUNK], U32, name="x_codes%d%d" % (g, c), align_bytes=64) for c in range(CHUNKS)] for g in range(PASSES)]
-        x_scales = [[keep.tile([P, CHUNK], U8, name="x_scales%d%d" % (g, c), align_bytes=64) for c in range(CHUNKS)] for g in range(PASSES)]
-        bias = keep.tile([P, HALVES, E + 1], F32, name="bias")
+        x_bf = [keep.tile([P, 2 * PACK * T], BF16, name="x_bf%d" % g, align_bytes=64) for g in range(PASSES)]
+        x_codes = {}
+        x_scales = {}
+        for g, c in UNITS:
+            x_codes[g, c] = keep.tile([P, CHUNK], U32, name="x_codes%d%d" % (g, c), align_bytes=64)
+            x_scales[g, c] = keep.tile([P, CHUNK], U8, name="x_scales%d%d" % (g, c), align_bytes=64)
+        xs_codes = [keep.tile([P, T], U32, name="xs_codes%d" % g, align_bytes=64) for g in range(PASSES)]
+        scale_tile = [keep.tile([P, T], U8, name="scale_tile%d" % i, align_bytes=64) for i in range(SCALE_TILES)]
+        xs_scales = [scale_tile[SHARED % SCALE_TILES][4 * g :, :] for g in range(PASSES)]
         y = [keep.tile([P, SLOTS], F32, name="y%d" % h) for h in range(HALVES)]
         ys = [keep.tile([P, T], F32, name="ys%d" % h) for h in range(HALVES)]
-        ring = [keep.tile([P, PASSES * 4 * N], F32, name="ring%d" % i, align_bytes=64) for i in range(RING)]
-        first = [keep.tile([P, PASSES * 4 * N], F32, name="first%d" % i, align_bytes=64) for i in range(2)]
-        prod = [[x_raw[h][r // 2][:, r % 2, :] for r in range(TOP)] for h in range(HALVES)]
+        ring = [keep.tile([P, PASSES * PACK * N], F32, name="ring%d" % i, align_bytes=64) for i in range(RING)]
+        early = [keep.tile([P, PASSES * PACK * N], F32, name="early%d" % i, align_bytes=64) for i in range(EARLY_UNITS)]
 
-        xs_codes = [keep.tile([P, T], U32, name="xs_codes%d" % g, align_bytes=64) for g in range(PASSES)]
-        spare = [first[1], ring[(E - 8) % RING], ring[(E - 7) % RING]]
+        gated = [[x_raw[h][r // 2][:, r % 2, :] for r in range(TOP)] for h in range(HALVES)]
+        gate_homes = (early[1], ring[(E - RING) % RING], ring[(E - RING + 1) % RING])
         gate_sb = {}
         for i, (h, r) in enumerate(FETCH_ORDER):
-            gate_sb[h, r] = spare[i // 3][:, i % 3 * T : (i % 3 + 1) * T]
+            gate_sb[h, r] = gate_homes[i // 3][:, i % 3 * T : (i % 3 + 1) * T]
+        turned = [ring[(E - RING + 2 + h) % RING] for h in range(HALVES)]
+
         x_rows = xT.rearrange("(g p u e) t -> g u p e t", g=PASSES, p=P, u=2, e=2)
-        w_rows = w.rearrange("x (g p j) n -> x g p (j n)", g=PASSES, p=P, j=4)
-        planes = [keep.tile([P, T], U8, name="planes%d" % i, align_bytes=64) for i in range(PLANE_TILES)]
-        xs_scales = [planes[E % PLANE_TILES][4 * g :, :] for g in range(PASSES)]
+        w_rows = w.rearrange("x (g p j) n -> x g p (j n)", g=PASSES, p=P, j=PACK)
+        b_cols = b.rearrange("(h p) x -> p h x", p=P)
         w_bf = {}
         w_codes = {}
         w_scales = {}
+        bias = {}
+
+        def load_bias(name, halves, e0, e1):
+            columns = keep.tile([P, halves.stop - halves.start, e1 - e0], F32, name=name)
+            nc.sync.dma_start(columns[:], b_cols[:, halves, e0:e1])
+            for h in range(halves.start, halves.stop):
+                for e in range(e0, e1):
+                    bias[e, h] = columns[:, h - halves.start, e - e0 : e - e0 + 1]
 
         def load_x(g, u):
             nc.sync.dma_start(x_raw[g][u][:], x_rows[g, u])
 
         def w_raw(e, g):
-            home = ring[e % RING] if e < E else first[0]
-            return home[:, g * 4 * N : (g + 1) * 4 * N]
+            home = early[0] if e == SHARED else ring[e % RING]
+            return home[:, g * PACK * N : (g + 1) * PACK * N]
+
+        def load_w_pass(e, g):
+            nc.sync.dma_start(w_raw(e, g), w_rows[e, g])
 
         def load_w(e):
             for g in range(PASSES):
-                nc.sync.dma_start(w_raw(e, g), w_rows[e, g])
+                load_w_pass(e, g)
+            for c, after in enumerate(BIAS_AFTER):
+                if after == e:
+                    e0 = c * CHUNK_EXPERTS
+                    e1 = e0 + CHUNK_EXPERTS
+                    if e0 < LATE:
+                        load_bias("bias%d" % c, slice(0, HALVES), e0, e1)
+                    else:
+                        load_bias("bias%d" % c, slice(1, HALVES), e0, e1 + 1 if e1 == E else e1)
 
-        def cast_x(g, u, on_vector):
-            dst = x_bf[g][:, 2 * T * u : 2 * T * (u + 1)].rearrange("p (c i e) -> p c e i", i=4, e=2)
-            src = x_raw[g][u][:].rearrange("p e (c i) -> p c e i", i=4)
-            if on_vector:
-                nc.vector.tensor_copy(dst, src)
-            else:
-                nc.scalar.copy(dst, src)
+        def round_x(g, u, copy):
+            copy(
+                x_bf[g][:, 2 * T * u : 2 * T * (u + 1)].rearrange("p (c i e) -> p c e i", i=4, e=2),
+                x_raw[g][u][:].rearrange("p e (c i) -> p c e i", i=4),
+            )
 
-        def group_shared_x(g):
-            dst = x_bf[g][:, 4 * T : 8 * T].rearrange("p (t u e) -> p t u e", u=2, e=2)
-            src = x_bf[g][:, 0 : 4 * T].rearrange("p (u t e) -> p t u e", u=2, e=2)
-            nc.vector.tensor_copy(dst, src)
+        def interleave_shared_x(g):
+            nc.vector.tensor_copy(
+                x_bf[g][:, PACK * T : 2 * PACK * T].rearrange("p (t u e) -> p t u e", u=2, e=2),
+                x_bf[g][:, 0 : PACK * T].rearrange("p (u t e) -> p t u e", u=2, e=2),
+            )
 
         def quantize_shared_x(g):
-            for t0, t1 in ((0, 512), (512, T)):
+            for t0, t1 in TOKEN_RANGES:
                 nc.vector.quantize_mx(
                     out=xs_codes[g][:, t0:t1].bitcast(FP8X4),
                     scales=xs_scales[g][:, t0:t1],
-                    in_=x_bf[g][:, 4 * T + 4 * t0 : 4 * T + 4 * t1],
+                    in_=x_bf[g][:, PACK * (T + t0) : PACK * (T + t1)],
                 )
 
-        def gathered(k):
-            home = first[k] if k < 2 else ring[PACE[k - 2] % RING]
-            return home[:].rearrange("p (q m) -> p q m", q=4)[:, 0:4:3, :]
+        def gathered(unit):
+            home = early[unit] if unit < EARLY_UNITS else ring[PACE[unit - EARLY_UNITS] % RING]
+            return home[:, 0 : 2 * CHUNK].rearrange("p (u s) -> p u s", u=2)
 
-        def grouped(k):
-            home = first[1 - k] if k < 1 else ring[PACE[k - 1] % RING]
-            return home[:, CHUNK : 3 * CHUNK].bitcast(BF16)
+        def interleaved(unit):
+            home = early[1] if unit == 0 else ring[PACE[unit - 1] % RING]
+            return home[:, 2 * CHUNK : 4 * CHUNK].bitcast(BF16)
 
-        def gather_x(k, u, pieces, width):
-            g, c = UNITS[k]
+        def gather_x(unit, u, entries, width):
+            g, c = UNITS[unit]
             window = x_bf[g][:].bitcast(U32)[:, T * u : T * u + width]
-            size = CHUNK // pieces
-            for s0 in range(0, CHUNK, size):
-                columns = offs_sb[:, (c * CHUNK + s0) // 16 : (c * CHUNK + s0 + size) // 16]
-                nc.vector.tensor_copy(gathered(k)[:, u, s0 : s0 + size].bitcast(U32), window.indirect(columns))
+            for s0 in range(0, CHUNK, entries):
+                m0 = c * CHUNK + s0
+                columns = offs_sb[:, m0 // LIST_COLUMN : (m0 + entries) // LIST_COLUMN]
+                nc.vector.tensor_copy(gathered(unit)[:, u, s0 : s0 + entries].bitcast(U32), window.indirect(columns))
 
-        def group_x(k):
+        def interleave_x(unit):
             nc.vector.tensor_copy(
-                grouped(k).rearrange("p (s u e) -> p s u e", u=2, e=2),
-                gathered(k).bitcast(BF16).rearrange("p u (s e) -> p s u e", e=2),
+                interleaved(unit).rearrange("p (s u e) -> p s u e", u=2, e=2),
+                gathered(unit).bitcast(BF16).rearrange("p u (s e) -> p s u e", e=2),
             )
 
-        def quantize_x(k):
-            g, c = UNITS[k]
-            nc.vector.quantize_mx(out=x_codes[g][c][:].bitcast(FP8X4), scales=x_scales[g][c][:], in_=grouped(k))
+        def quantize_x(unit):
+            nc.vector.quantize_mx(
+                out=x_codes[UNITS[unit]][:].bitcast(FP8X4), scales=x_scales[UNITS[unit]][:], in_=interleaved(unit)
+            )
 
-        def cast_w(e):
-            w_bf[e] = wbf_pool.tile([P, PASSES, 4 * N], BF16, name="w_bf", align_bytes=64)
+        def round_w(e):
+            w_bf[e] = wbf_pool.tile([P, PASSES, PACK * N], BF16, name="w_bf", align_bytes=64)
             for g in range(PASSES):
-                dst = w_bf[e][:, g, :].rearrange("p (c i j) -> p c j i", i=4, j=4)
-                src = w_raw(e, g).rearrange("p (j c i) -> p c j i", j=4, i=4)
-                if (e, g) in VECTOR_CASTS:
-                    nc.vector.tensor_copy(dst, src)
-                else:
-                    nc.scalar.copy(dst, src)
+                copy = nc.vector.tensor_copy if (e, g) in VECTOR_ROUNDS else nc.scalar.copy
+                copy(
+                    w_bf[e][:, g, :].rearrange("p (c i j) -> p c j i", i=4, j=PACK),
+                    w_raw(e, g).rearrange("p (j c i) -> p c j i", j=PACK, i=4),
+                )
 
         def quantize_w(e):
             w_codes[e] = wq_pool.tile([P, PASSES * N], U32, name="w_codes", align_bytes=64)
-            w_scales[e] = planes[e % PLANE_TILES][4 * (e // PLANE_TILES % 4) :, 0 : PASSES * N]
+            w_scales[e] = scale_tile[e % SCALE_TILES][4 * (e // SCALE_TILES % 4) :, 0 : PASSES * N]
             nc.vector.quantize_mx(
-                out=w_codes[e][:].bitcast(FP8X4),
-                scales=w_scales[e],
-                in_=w_bf[e][:].rearrange("p g m -> p (g m)"),
+                out=w_codes[e][:].bitcast(FP8X4), scales=w_scales[e], in_=w_bf[e][:].rearrange("p g m -> p (g m)")
             )
 
         def product(acc, e, h, codes, scales, cols):
@@ -169,125 +212,132 @@ def tile_moe_shr_lin_gelu_kernel(tc, xT, w, b, gate, offs, pos1, pos2, pos3, pos
                     stop=(g == PASSES - 1),
                 )
 
-        def expert(e):
-            c, place = divmod(e, EXPERTS_PER_CHUNK)
-            acc = bank[e % 8][:].rearrange("p (h c) -> p h c", c=C)
-            codes = [x_codes[g][c] for g in range(PASSES)]
-            scales = [x_scales[g][c] for g in range(PASSES)]
-            for h in range(HALVES):
-                product(acc[:, h, :], e, h, codes, scales, slice(place * C, (place + 1) * C))
-            for h in range(HALVES):
-                nc.scalar.activation(y[h][:, e * C : (e + 1) * C], acc[:, h, :], GELU, bias=bias[:, h, e : e + 1])
+        def routed_sums(e, h):
+            return bank[e % BANKS][:, h * C : (h + 1) * C]
 
-        def shared_expert():
+        def routed_products(e):
+            c, place = divmod(e, CHUNK_EXPERTS)
+            codes = [x_codes[g, c] for g in range(PASSES)]
+            scales = [x_scales[g, c] for g in range(PASSES)]
             for h in (1, 0):
-                for i, (t0, t1) in enumerate(TOKEN_RANGES):
-                    acc_s = bank[4 + 2 * (1 - h) + i]
-                    product(acc_s[:, 0 : t1 - t0], E, h, xs_codes, xs_scales, slice(t0, t1))
-                    nc.scalar.activation(ys[h][:, t0:t1], acc_s[:, 0 : t1 - t0], GELU, bias=bias[:, h, E : E + 1])
+                product(routed_sums(e, h), e, h, codes, scales, slice(place * C, (place + 1) * C))
+
+        def routed_gelu(e, h):
+            nc.scalar.activation(y[h][:, e * C : (e + 1) * C], routed_sums(e, h), GELU, bias=bias[e, h])
+
+        def fetch(h, r, t0, t1):
+            columns = pos_sb[r][:, t0 // LIST_COLUMN : t1 // LIST_COLUMN]
+            nc.vector.tensor_tensor(gated[h][r][:, t0:t1], y[h][:].indirect(columns), gate_sb[h, r][:, t0:t1], MULT)
+
+        def add_transposed(sums, term, is_first, is_last):
+            for (t0, t1), acc in zip(TOKEN_RANGES, sums):
+                for t in range(t0, t1, P):
+                    nc.tensor.matmul(
+                        acc[:, t - t0 : t - t0 + P],
+                        term[:, t : t + P],
+                        ident[:],
+                        start=is_first and t == t0,
+                        stop=is_last and t == t1 - P,
+                        is_transpose=True,
+                    )
+
+        def transpose_back(sums, staging, totals):
+            for (t0, t1), acc, total in zip(TOKEN_RANGES, sums, totals):
+                nc.scalar.copy(staging[:, t0:t1], acc[:, 0 : t1 - t0])
+                for t in range(t0, t1, P):
+                    nc.tensor.transpose(total[:, t - t0 : t - t0 + P], staging[:, t : t + P], ident[:])
 
         load_x(0, 0)
         nc.sync.dma_start(offs_sb[:], offs)
         load_x(0, 1)
         load_w(0)
-        load_w(1)
+        load_w_pass(1, 0)
         load_x(1, 0)
+        load_w_pass(1, 1)
         load_x(1, 1)
-        nc.sync.dma_start(bias[:], b.rearrange("(h p) e -> p h e", p=P))
         for e in range(2, RING):
             load_w(e)
 
-        cast_x(0, 0, True)
-        cast_x(0, 1, False)
-        gather_x(0, 0, 2, T)
-        cast_w(0)
-        cast_w(1)
-        cast_x(1, 0, False)
-        cast_x(1, 1, False)
-        gather_x(0, 1, 2, T)
-        group_shared_x(0)
-        gather_x(1, 0, 1, WINDOW)
-        group_x(0)
+        round_x(0, 0, nc.vector.tensor_copy)
+        round_x(0, 1, nc.scalar.copy)
+        gather_x(0, 0, CHUNK // 2, T)
+        gather_x(1, 0, CHUNK // 2, T)
+        round_w(0)
+        round_w(1)
+        round_x(1, 0, nc.vector.tensor_copy)
+        round_x(1, 1, nc.scalar.copy)
+        interleave_shared_x(0)
+        gather_x(0, 1, CHUNK, WIDE_WINDOW)
+        gather_x(1, 1, CHUNK, WIDE_WINDOW)
+        interleave_x(0)
         quantize_w(0)
-        gather_x(1, 1, 1, WINDOW)
         quantize_x(0)
         quantize_w(1)
-        group_shared_x(1)
+        interleave_shared_x(1)
 
-        loaded = RING
+        next_load = RING
         for e in range(2, E):
-            cast_w(e)
-            k = PACE.index(e) + 2 if e in PACE else None
-            if k is not None and k < len(UNITS):
-                gather_x(k, 0, 1, WINDOW)
-            quantize_w(e)
-            if k is not None:
-                group_x(k - 1)
-                if k < len(UNITS):
-                    gather_x(k, 1, 1, WINDOW)
-                quantize_x(k - 1)
+            round_w(e)
+            if e in PACE:
+                unit = PACE.index(e) + EARLY_UNITS
+                if unit < len(UNITS):
+                    for u in range(2):
+                        gather_x(unit, u, CHUNK, WIDE_WINDOW)
+                interleave_x(unit - 1)
+                quantize_w(e)
+                quantize_x(unit - 1)
+            else:
+                quantize_w(e)
             for j in range(E):
-                if PRODUCT_AFTER[j] == e:
-                    assert j <= e < j + 4 * PLANE_TILES and all(PACE[k - 1] <= e for k in range(1, len(UNITS)) if UNITS[k][1] == j // EXPERTS_PER_CHUNK)
-                    expert(j)
-            while loaded < E:
-                old = loaded - RING
-                last_use = PACE[min(PACE.index(old) + 1, len(PACE) - 1)] if old in PACE else old
-                if last_use > e:
+                if product_step[j] == e:
+                    routed_products(j)
+            for j in range(E):
+                if gelu_step[j] == e:
+                    routed_gelu(j, 1)
+                    if j < LATE:
+                        routed_gelu(j, 0)
+            while next_load < E:
+                old = next_load - RING
+                if (PACE[PACE.index(old) + 1] if old in PACE else old) > e:
                     break
-                load_w(loaded)
-                loaded += 1
-            if e == 4:
-                for r, p_list in enumerate((pos1, pos2, pos3, pos4)):
-                    nc.sync.dma_start(pos_sb[r][:], p_list)
-
-        def load_gate(h, r):
-            nc.sync.dma_start(gate_sb[h, r], gate[r, h * P : (h + 1) * P, :])
-
-        def fetch(h, r, t0, t1):
-            nc.vector.tensor_tensor(
-                prod[h][r][:, t0:t1], y[h][:].indirect(pos_sb[r][:, t0 // 16 : t1 // 16]), gate_sb[h, r][:, t0:t1], MULT
-            )
-
-        def add(dst, a, c):
-            nc.vector.tensor_tensor(dst, a, c, ADD)
-
-        def add_turned(sums, term, first_term, last_term):
-            for (t0, t1), acc_t in zip(TOKEN_RANGES, sums):
-                for t in range(t0, t1, P):
-                    nc.tensor.matmul(
-                        acc_t[:, t - t0 : t - t0 + P], term[:, t : t + P], ident[:],
-                        start=first_term and t == t0, stop=last_term and t == t1 - P, is_transpose=True,
-                    )
-
-        def turn_back(sums, turned, back):
-            for (t0, t1), acc_t, total in zip(TOKEN_RANGES, sums, back):
-                nc.scalar.copy(turned[:, t0:t1], acc_t[:, 0 : t1 - t0])
-                for t in range(t0, t1, P):
-                    nc.tensor.transpose(total[:, t - t0 : t - t0 + P], turned[:, t : t + P], ident[:])
+                load_w(next_load)
+                next_load += 1
+            if e == LISTS_AFTER:
+                for r, positions in enumerate((pos1, pos2, pos3, pos4)):
+                    nc.sync.dma_start(pos_sb[r][:], positions)
 
         for i, (h, r) in enumerate(FETCH_ORDER):
-            if i == 0:
-                load_w(E)
-            load_gate(h, r)
-        quantize_shared_x(0)
-        quantize_shared_x(1)
-        cast_w(E)
-        quantize_w(E)
-        shared_expert()
-        back = {1: (bank[4], bank[5]), 0: (bank[6], bank[7])}
+            if i == SHARED_BEFORE_GATE:
+                load_w(SHARED)
+            if i == LATE_BIAS_BEFORE_GATE:
+                load_bias("bias_late", slice(0, 1), LATE, SHARED + 1)
+            nc.sync.dma_start(gate_sb[h, r], gate[r, h * P : (h + 1) * P, :])
+        for e in range(E - 2, LATE - 1, -2):
+            routed_gelu(e, 0)
+            routed_gelu(e + 1, 0)
+
+        for g in range(PASSES):
+            quantize_shared_x(g)
+        round_w(SHARED)
+        quantize_w(SHARED)
+        totals = {1: bank[4:6], 0: bank[6:8]}
         for h in (1, 0):
-            sums = (bank[2 * h], bank[2 * h + 1])
-            terms = [prod[h][0], prod[h][1], prod[h][2], ys[h]] if h == 1 else [prod[h][0], ys[h], prod[h][1], prod[h][2]]
+            for (t0, t1), acc in zip(TOKEN_RANGES, totals[h]):
+                product(acc[:, 0 : t1 - t0], SHARED, h, xs_codes, xs_scales, slice(t0, t1))
+                nc.scalar.activation(ys[h][:, t0:t1], acc[:, 0 : t1 - t0], GELU, bias=bias[SHARED, h])
+
+        for h in (1, 0):
+            sums = bank[2 * h : 2 * h + 2]
             for r in range(TOP - 1):
                 fetch(h, r, 0, T)
+            terms = gated[h][0:3] + [ys[h]] if h == 1 else [gated[h][0], ys[h]] + gated[h][1:3]
             for i, term in enumerate(terms):
-                add_turned(sums, term, i == 0, i == len(terms) - 1)
-            turn_back(sums, ring[(E - 6 + h) % RING], back[h])
+                add_transposed(sums, term, i == 0, i == len(terms) - 1)
+            transpose_back(sums, turned[h], totals[h])
         fetch(1, TOP - 1, 0, T)
         for t0, t1 in TOKEN_RANGES:
             fetch(0, TOP - 1, t0, t1)
         for h in (1, 0):
-            for (t0, t1), total in zip(TOKEN_RANGES, back[h]):
-                add(ys[h][:, t0:t1], total[:, 0 : t1 - t0], prod[h][3][:, t0:t1])
+            for (t0, t1), total in zip(TOKEN_RANGES, totals[h]):
+                nc.vector.tensor_tensor(ys[h][:, t0:t1], total[:, 0 : t1 - t0], gated[h][TOP - 1][:, t0:t1], ADD)
                 nc.sync.dma_start(out[h * P : (h + 1) * P, t0:t1], ys[h][:, t0:t1])

from contextlib import ExitStack

import concourse.mybir as mybir
from concourse.masks import make_identity

K, T, E, C, N = 1024, 640, 20, 128, 256
TOP = 4
SLOTS = E * C
SHARED = E
FLOPS = 2 * K * N * (SLOTS + T)

F32 = mybir.dt.float32
BF16 = mybir.dt.bfloat16
U32 = mybir.dt.uint32
U16 = mybir.dt.uint16
U8 = mybir.dt.uint8
FP8X4 = mybir.dt.float8_e4m3fn_x4
GELU = mybir.ActivationFunctionType.Gelu_apprx_tanh
MULT = mybir.AluOpType.mult
ADD = mybir.AluOpType.add

P = 128
PACK = 4
PASSES = K // (P * PACK)
HALVES = N // P
LIST_COLUMN = 16
BANKS = 8
BANK = 512
TOKEN_RANGES = ((0, BANK), (BANK, T))

CHUNK = 512
CHUNK_EXPERTS = CHUNK // C
WIDE_WINDOW = 1024
UNITS = ((0, 0), (0, 1), (1, 0), (1, 1), (0, 2), (1, 2), (0, 3), (1, 3), (0, 4), (1, 4))
EARLY_UNITS = 2

RING = 8
BF16_BUFFERS = 6
SCALE_TILES = 3
PACE = (2, 4, 5, 6, 9, 10, 11, 12, 18)
VECTOR_ROUNDS = ((2, 0), (9, 1), (11, 1), (12, 1), (18, 0))
BIAS_AFTER = (10, 11, 16, 19, 19)
LATE = E - BANKS
LISTS_AFTER = 4
FETCH_ORDER = ((1, 0), (1, 1), (1, 2), (0, 0), (0, 1), (0, 2), (1, 3), (0, 3))
SHARED_BEFORE_GATE = 1
LATE_BIAS_BEFORE_GATE = 2


def tile_moe_shr_lin_gelu_kernel(tc, xT, w, b, gate, offs, pos1, pos2, pos3, pos4, out):
    nc = tc.nc

    chunk_ready = [max(PACE[u - 1] for u in range(1, len(UNITS)) if UNITS[u][1] == c) for c in range(SLOTS // CHUNK)]
    product_step = []
    gelu_step = []
    for j in range(E):
        bank_free = gelu_step[j - BANKS] + 1 if j >= BANKS else 0
        product_step.append(max(j, chunk_ready[j // CHUNK_EXPERTS], bank_free))
        gelu_step.append(max(product_step[j], BIAS_AFTER[j // CHUNK_EXPERTS]))
    assert max(gelu_step) < E and all(product_step[j] < j + 4 * SCALE_TILES for j in range(E))

    with ExitStack() as ctx:
        lists = ctx.enter_context(tc.tile_pool(name="lists", bufs=1))
        keep = ctx.enter_context(tc.tile_pool(name="keep", bufs=1))
        wbf_pool = ctx.enter_context(tc.tile_pool(name="wbf", bufs=BF16_BUFFERS))
        wq_pool = ctx.enter_context(tc.tile_pool(name="wq", bufs=4 * SCALE_TILES))
        psum = ctx.enter_context(tc.psum_pool(name="psum", bufs=1))
        bank = [psum.tile([P, BANK], F32, name="bank%d" % i) for i in range(BANKS)]

        offs_sb = lists.tile([P, SLOTS // LIST_COLUMN], U16, name="offs_sb")
        pos_sb = [lists.tile([P, T // LIST_COLUMN], U16, name="pos_sb%d" % r) for r in range(TOP)]

        warm = keep.tile([P, 8], F32, name="warm")
        warm_out = keep.tile([P, 8], F32, name="warm_out")
        nc.vector.memset(warm[:], 0.0)
        nc.scalar.activation(warm_out[:], warm[:], GELU)
        ident = keep.tile([P, P], F32, name="ident")
        make_identity(nc, ident[:])

        x_raw = [[keep.tile([P, 2, T], F32, name="x_raw%d%d" % (g, u)) for u in range(2)] for g in range(PASSES)]
        x_bf = [keep.tile([P, 2 * PACK * T], BF16, name="x_bf%d" % g, align_bytes=64) for g in range(PASSES)]
        x_codes = {}
        x_scales = {}
        for g, c in UNITS:
            x_codes[g, c] = keep.tile([P, CHUNK], U32, name="x_codes%d%d" % (g, c), align_bytes=64)
            x_scales[g, c] = keep.tile([P, CHUNK], U8, name="x_scales%d%d" % (g, c), align_bytes=64)
        xs_codes = [keep.tile([P, T], U32, name="xs_codes%d" % g, align_bytes=64) for g in range(PASSES)]
        scale_tile = [keep.tile([P, T], U8, name="scale_tile%d" % i, align_bytes=64) for i in range(SCALE_TILES)]
        xs_scales = [scale_tile[SHARED % SCALE_TILES][4 * g :, :] for g in range(PASSES)]
        y = [keep.tile([P, SLOTS], F32, name="y%d" % h) for h in range(HALVES)]
        ys = [keep.tile([P, T], F32, name="ys%d" % h) for h in range(HALVES)]
        ring = [keep.tile([P, PASSES * PACK * N], F32, name="ring%d" % i, align_bytes=64) for i in range(RING)]
        early = [keep.tile([P, PASSES * PACK * N], F32, name="early%d" % i, align_bytes=64) for i in range(EARLY_UNITS)]

        gated = [[x_raw[h][r // 2][:, r % 2, :] for r in range(TOP)] for h in range(HALVES)]
        gate_homes = (early[1], ring[(E - RING) % RING], ring[(E - RING + 1) % RING])
        gate_sb = {}
        for i, (h, r) in enumerate(FETCH_ORDER):
            gate_sb[h, r] = gate_homes[i // 3][:, i % 3 * T : (i % 3 + 1) * T]
        turned = [ring[(E - RING + 2 + h) % RING] for h in range(HALVES)]

        x_rows = xT.rearrange("(g p u e) t -> g u p e t", g=PASSES, p=P, u=2, e=2)
        w_rows = w.rearrange("x (g p j) n -> x g p (j n)", g=PASSES, p=P, j=PACK)
        b_cols = b.rearrange("(h p) x -> p h x", p=P)
        w_bf = {}
        w_codes = {}
        w_scales = {}
        bias = {}

        def load_bias(name, halves, e0, e1):
            columns = keep.tile([P, halves.stop - halves.start, e1 - e0], F32, name=name)
            nc.sync.dma_start(columns[:], b_cols[:, halves, e0:e1])
            for h in range(halves.start, halves.stop):
                for e in range(e0, e1):
                    bias[e, h] = columns[:, h - halves.start, e - e0 : e - e0 + 1]

        def load_x(g, u):
            nc.sync.dma_start(x_raw[g][u][:], x_rows[g, u])

        def w_raw(e, g):
            home = early[0] if e == SHARED else ring[e % RING]
            return home[:, g * PACK * N : (g + 1) * PACK * N]

        def load_w_pass(e, g):
            nc.sync.dma_start(w_raw(e, g), w_rows[e, g])

        def load_w(e):
            for g in range(PASSES):
                load_w_pass(e, g)
            for c, after in enumerate(BIAS_AFTER):
                if after == e:
                    e0 = c * CHUNK_EXPERTS
                    e1 = e0 + CHUNK_EXPERTS
                    if e0 < LATE:
                        load_bias("bias%d" % c, slice(0, HALVES), e0, e1)
                    else:
                        load_bias("bias%d" % c, slice(1, HALVES), e0, e1 + 1 if e1 == E else e1)

        def round_x(g, u, copy):
            copy(
                x_bf[g][:, 2 * T * u : 2 * T * (u + 1)].rearrange("p (c i e) -> p c e i", i=4, e=2),
                x_raw[g][u][:].rearrange("p e (c i) -> p c e i", i=4),
            )

        def interleave_shared_x(g):
            nc.vector.tensor_copy(
                x_bf[g][:, PACK * T : 2 * PACK * T].rearrange("p (t u e) -> p t u e", u=2, e=2),
                x_bf[g][:, 0 : PACK * T].rearrange("p (u t e) -> p t u e", u=2, e=2),
            )

        def quantize_shared_x(g):
            for t0, t1 in TOKEN_RANGES:
                nc.vector.quantize_mx(
                    out=xs_codes[g][:, t0:t1].bitcast(FP8X4),
                    scales=xs_scales[g][:, t0:t1],
                    in_=x_bf[g][:, PACK * (T + t0) : PACK * (T + t1)],
                )

        def gathered(unit):
            home = early[unit] if unit < EARLY_UNITS else ring[PACE[unit - EARLY_UNITS] % RING]
            return home[:, 0 : 2 * CHUNK].rearrange("p (u s) -> p u s", u=2)

        def interleaved(unit):
            home = early[1] if unit == 0 else ring[PACE[unit - 1] % RING]
            return home[:, 2 * CHUNK : 4 * CHUNK].bitcast(BF16)

        def gather_x(unit, u, entries, width):
            g, c = UNITS[unit]
            window = x_bf[g][:].bitcast(U32)[:, T * u : T * u + width]
            for s0 in range(0, CHUNK, entries):
                m0 = c * CHUNK + s0
                columns = offs_sb[:, m0 // LIST_COLUMN : (m0 + entries) // LIST_COLUMN]
                nc.vector.tensor_copy(gathered(unit)[:, u, s0 : s0 + entries].bitcast(U32), window.indirect(columns))

        def interleave_x(unit):
            nc.vector.tensor_copy(
                interleaved(unit).rearrange("p (s u e) -> p s u e", u=2, e=2),
                gathered(unit).bitcast(BF16).rearrange("p u (s e) -> p s u e", e=2),
            )

        def quantize_x(unit):
            nc.vector.quantize_mx(
                out=x_codes[UNITS[unit]][:].bitcast(FP8X4), scales=x_scales[UNITS[unit]][:], in_=interleaved(unit)
            )

        def round_w(e):
            w_bf[e] = wbf_pool.tile([P, PASSES, PACK * N], BF16, name="w_bf", align_bytes=64)
            for g in range(PASSES):
                copy = nc.vector.tensor_copy if (e, g) in VECTOR_ROUNDS else nc.scalar.copy
                copy(
                    w_bf[e][:, g, :].rearrange("p (c i j) -> p c j i", i=4, j=PACK),
                    w_raw(e, g).rearrange("p (j c i) -> p c j i", j=PACK, i=4),
                )

        def quantize_w(e):
            w_codes[e] = wq_pool.tile([P, PASSES * N], U32, name="w_codes", align_bytes=64)
            w_scales[e] = scale_tile[e % SCALE_TILES][4 * (e // SCALE_TILES % 4) :, 0 : PASSES * N]
            nc.vector.quantize_mx(
                out=w_codes[e][:].bitcast(FP8X4), scales=w_scales[e], in_=w_bf[e][:].rearrange("p g m -> p (g m)")
            )

        def product(acc, e, h, codes, scales, cols):
            for g in range(PASSES):
                m = slice(g * N + h * P, g * N + (h + 1) * P)
                nc.tensor.matmul_mx(
                    out=acc,
                    lhsT=w_codes[e][:, m].bitcast(FP8X4),
                    lhsT_scale=w_scales[e][:, m],
                    rhs=codes[g][:, cols].bitcast(FP8X4),
                    rhs_scale=scales[g][:, cols],
                    start=(g == 0),
                    stop=(g == PASSES - 1),
                )

        def routed_sums(e, h):
            return bank[e % BANKS][:, h * C : (h + 1) * C]

        def routed_products(e):
            c, place = divmod(e, CHUNK_EXPERTS)
            codes = [x_codes[g, c] for g in range(PASSES)]
            scales = [x_scales[g, c] for g in range(PASSES)]
            for h in (1, 0):
                product(routed_sums(e, h), e, h, codes, scales, slice(place * C, (place + 1) * C))

        def routed_gelu(e, h):
            nc.scalar.activation(y[h][:, e * C : (e + 1) * C], routed_sums(e, h), GELU, bias=bias[e, h])

        def fetch(h, r, t0, t1):
            columns = pos_sb[r][:, t0 // LIST_COLUMN : t1 // LIST_COLUMN]
            nc.vector.tensor_tensor(gated[h][r][:, t0:t1], y[h][:].indirect(columns), gate_sb[h, r][:, t0:t1], MULT)

        def add_transposed(sums, term, is_first, is_last):
            for (t0, t1), acc in zip(TOKEN_RANGES, sums):
                for t in range(t0, t1, P):
                    nc.tensor.matmul(
                        acc[:, t - t0 : t - t0 + P],
                        term[:, t : t + P],
                        ident[:],
                        start=is_first and t == t0,
                        stop=is_last and t == t1 - P,
                        is_transpose=True,
                    )

        def transpose_back(sums, staging, totals):
            for (t0, t1), acc, total in zip(TOKEN_RANGES, sums, totals):
                nc.scalar.copy(staging[:, t0:t1], acc[:, 0 : t1 - t0])
                for t in range(t0, t1, P):
                    nc.tensor.transpose(total[:, t - t0 : t - t0 + P], staging[:, t : t + P], ident[:])

        load_x(0, 0)
        nc.sync.dma_start(offs_sb[:], offs)
        load_x(0, 1)
        load_w(0)
        load_w_pass(1, 0)
        load_x(1, 0)
        load_w_pass(1, 1)
        load_x(1, 1)
        for e in range(2, RING):
            load_w(e)

        round_x(0, 0, nc.vector.tensor_copy)
        round_x(0, 1, nc.scalar.copy)
        gather_x(0, 0, CHUNK // 2, T)
        gather_x(1, 0, CHUNK // 2, T)
        round_w(0)
        round_w(1)
        round_x(1, 0, nc.vector.tensor_copy)
        round_x(1, 1, nc.scalar.copy)
        interleave_shared_x(0)
        gather_x(0, 1, CHUNK, WIDE_WINDOW)
        gather_x(1, 1, CHUNK, WIDE_WINDOW)
        interleave_x(0)
        quantize_w(0)
        quantize_x(0)
        quantize_w(1)
        interleave_shared_x(1)

        next_load = RING
        for e in range(2, E):
            round_w(e)
            if e in PACE:
                unit = PACE.index(e) + EARLY_UNITS
                if unit < len(UNITS):
                    for u in range(2):
                        gather_x(unit, u, CHUNK, WIDE_WINDOW)
                interleave_x(unit - 1)
                quantize_w(e)
                quantize_x(unit - 1)
            else:
                quantize_w(e)
            for j in range(E):
                if product_step[j] == e:
                    routed_products(j)
            for j in range(E):
                if gelu_step[j] == e:
                    routed_gelu(j, 1)
                    if j < LATE:
                        routed_gelu(j, 0)
            while next_load < E:
                old = next_load - RING
                if (PACE[PACE.index(old) + 1] if old in PACE else old) > e:
                    break
                load_w(next_load)
                next_load += 1
            if e == LISTS_AFTER:
                for r, positions in enumerate((pos1, pos2, pos3, pos4)):
                    nc.sync.dma_start(pos_sb[r][:], positions)

        for i, (h, r) in enumerate(FETCH_ORDER):
            if i == SHARED_BEFORE_GATE:
                load_w(SHARED)
            if i == LATE_BIAS_BEFORE_GATE:
                load_bias("bias_late", slice(0, 1), LATE, SHARED + 1)
            nc.sync.dma_start(gate_sb[h, r], gate[r, h * P : (h + 1) * P, :])
        for e in range(E - 2, LATE - 1, -2):
            routed_gelu(e, 0)
            routed_gelu(e + 1, 0)

        for g in range(PASSES):
            quantize_shared_x(g)
        round_w(SHARED)
        quantize_w(SHARED)
        totals = {1: bank[4:6], 0: bank[6:8]}
        for h in (1, 0):
            for (t0, t1), acc in zip(TOKEN_RANGES, totals[h]):
                product(acc[:, 0 : t1 - t0], SHARED, h, xs_codes, xs_scales, slice(t0, t1))
                nc.scalar.activation(ys[h][:, t0:t1], acc[:, 0 : t1 - t0], GELU, bias=bias[SHARED, h])

        for h in (1, 0):
            sums = bank[2 * h : 2 * h + 2]
            for r in range(TOP - 1):
                fetch(h, r, 0, T)
            terms = gated[h][0:3] + [ys[h]] if h == 1 else [gated[h][0], ys[h]] + gated[h][1:3]
            for i, term in enumerate(terms):
                add_transposed(sums, term, i == 0, i == len(terms) - 1)
            transpose_back(sums, turned[h], totals[h])
        fetch(1, TOP - 1, 0, T)
        for t0, t1 in TOKEN_RANGES:
            fetch(0, TOP - 1, t0, t1)
        for h in (1, 0):
            for (t0, t1), total in zip(TOKEN_RANGES, totals[h]):
                nc.vector.tensor_tensor(ys[h][:, t0:t1], total[:, 0 : t1 - t0], gated[h][TOP - 1][:, t0:t1], ADD)
                nc.sync.dma_start(out[h * P : (h + 1) * P, t0:t1], ys[h][:, t0:t1])
